import numpy as np, ml_dtypes
CORES = [3,5,19,21,35,37,51,53,67,69]
N = 10
DEG, TK = 3, 512
MASK = [[0,3,1],[0,3,1],[0,3,2],[0,3,1],[0,3,4],[0,3,5],[0,3,6],[0,3,7],[0,3,8],[0,3,9]]
def setup_inputs(rng):
    return {"x": rng.standard_normal((N, 128, TK), dtype=np.float32).astype(ml_dtypes.bfloat16), "w": rng.standard_normal((N, 128, DEG * 128), dtype=np.float32).astype(ml_dtypes.bfloat16)}
def setup_inputs_big(rng):
    d = setup_inputs(rng)
    for k in ("x", "w"): d[k] = (d[k].astype(np.float32) * 1024.0).astype(d[k].dtype)
    return d
def setup_inputs_small(rng):
    d = setup_inputs(rng)
    for k in ("x", "w"): d[k] = (d[k].astype(np.float32) * (1 / 1024.0)).astype(d[k].dtype)
    return d
def setup_inputs_apart(rng):
    d = setup_inputs(rng)
    f = (10.0 ** rng.permutation(np.linspace(-1.5, 1.5, N))).astype(np.float32).reshape(N, 1, 1)
    for k in ("x", "w"): d[k] = (d[k].astype(np.float32) * f).astype(d[k].dtype)
    return d
def reference(x, w):
    X, W = x.astype(np.float64), w.astype(np.float64)
    y = np.zeros((N, 128, TK))
    for r in range(N):
        for i, j in enumerate(MASK[r]):
            y[r] += W[r][:, 128 * i:128 * i + 128].T @ X[j]
    return {"y": y.astype(ml_dtypes.bfloat16 if x.dtype != np.float64 else np.float64)}

@@ -1,0 +1,137 @@
+from concourse.bass import DstId, RemoteDMATransfer
+
+TILE = 128
+WAVE = 2
+
+SCRATCH = {
+    "xs": ("sbuf", [128, 512], "bfloat16"),
+    "ws": ("sbuf", [128, 384], "bfloat16"),
+    "l0": ("sbuf", [128, 512], "bfloat16"),
+    "l1": ("sbuf", [128, 512], "bfloat16"),
+    "l2": ("sbuf", [128, 512], "bfloat16"),
+    "ys": ("sbuf", [128, 512], "bfloat16"),
+    "acc": ("psum", [128, 512], "float32"),
+}
+SEMAPHORES = ["ldx", "ldw", "a0", "a1", "a2", "sent", "mm", "cp", "st"]
+
+
+def _bits(m):
+    return [e for e in range(m.bit_length()) if (m >> e) & 1]
+
+
+def _mask(es):
+    m = 0
+    for e in es:
+        m |= 1 << e
+    return m
+
+
+def _plan(T, topo):
+    cores, need = T.cores, T.tables["MASK"]
+    n = len(cores)
+    chip = [topo.chip(c) for c in cores]
+    users = {}
+    for j in range(n):
+        u = [r for r in range(n) if r != j and j in need[r]]
+        if u:
+            users[j] = u
+    far = {j: sorted(set(chip[r] for r in users[j]) - set([chip[j]])) for j in users}
+    gate = {}
+    for ch in sorted(set(chip)):
+        here = [r for r in range(n) if chip[r] == ch]
+        own = [r for r in here if r in users]
+        gate[ch] = min(own, key=lambda r: len(far[r])) if own else here[0]
+
+    calls = {r: [] for r in range(n)}
+    count, eta, relay = {}, {}, {r: [] for r in range(n)}
+    turn = 0
+    for j in sorted(users, key=lambda j: -len(far[j])):
+        src = cores[j]
+        near = [r for r in users[j] if chip[r] == chip[j]]
+        out = []
+        if far[j]:
+            out = _bits(topo.mask(src, cores[[r for r in users[j] if chip[r] != chip[j]][0]]))
+        cold = [ch for ch in far[j] if gate[ch] not in users]
+        warm = [ch for ch in far[j] if gate[ch] in users]
+        k = (WAVE * turn) % len(cold) if cold else 0
+        order = cold[k:] + cold[:k] + warm
+        turn += 1
+        for w in range(0, len(order), WAVE):
+            wave = order[w:w + WAVE]
+            per = len(out) // len(wave)
+            dests = []
+            for q, ch in enumerate(wave):
+                there = [r for r in users[j] if chip[r] == ch]
+                first = gate[ch] if gate[ch] in there else there[0]
+                es = out[q * per:(q + 1) * per]
+                dests.append((first, es))
+                count[(first, j)], eta[(first, j)] = len(es), 2.0 * (w // WAVE + 1)
+                rest = [r for r in there if r != first]
+                if rest:
+                    relay[first].append((eta[(first, j)], j, rest))
+            calls[j].append((j, dests))
+        for r in near:
+            es = [e for e in _bits(topo.mask(src, cores[r])) if e not in out]
+            calls[j].append((j, [(r, es)]))
+            count[(r, j)], eta[(r, j)] = len(es), 3.0
+    for f in range(n):
+        t = 0.0
+        for e0, j, rest in sorted(relay[f]):
+            t = max(t, e0) + 2.0
+            for r in rest:
+                es = _bits(topo.mask(cores[f], cores[r]))
+                if f in far and len(far[f]) > 1:
+                    busy = _bits(topo.mask(cores[f], cores[[u for u in users[f] if chip[u] != chip[f]][0]]))
+                    es = [e for e in es if e not in busy]
+                calls[f].append((j, [(r, es)]))
+                count[(r, j)], eta[(r, j)] = len(es), t
+    return calls, count, eta
+
+
+def rank_program(g, core, T, topo):
+    rank = T.rank_of(core)
+    if rank is None:
+        return
+    S = T.sem
+    need = T.tables["MASK"]
+    row = need[rank]
+    calls, count, eta = _plan(T, topo)
+
+    def held(j):
+        if j == rank:
+            return T.xs, S.ldx, 16
+        i = row.index(j)
+        return T["l%d" % i], S["a%d" % i], count[(rank, j)]
+
+    g.sync.dma_start(T.xs[:, :], T.x[:, :]).then_inc(S.ldx, 16)
+    g.sync.wait_ge(S.ldx, 16)
+    g.sync.dma_start(T.ws[:, :], T.w[:, :]).then_inc(S.ldw, 16)
+
+    sent = 0
+    for j, dests in calls[rank]:
+        buf, sem, val = held(j)
+        g.wait_ge(sem, val)
+        trs = []
+        for r, es in dests:
+            assert topo.may_write(core, T.cores[r])
+            rid, pid, _ = topo.addr(T.cores[r])
+            i = need[r].index(j)
+            trs.append(RemoteDMATransfer(dst_ids=[DstId(rid=rid, pnc=pid)], dma_engine_mask=_mask(es),
+                                         remote_sem=S["a%d" % i], src=buf[:, :], dst=T["l%d" % i][:, :]))
+            sent += len(es)
+        g.remote_dma_fused(trs, local_sem=S.sent)
+
+    order = sorted(range(len(row)), key=lambda i: 0.0 if row[i] == rank else eta[(rank, row[i])])
+    g.tensor.wait_ge(S.ldw, 16)
+    for k, i in enumerate(order):
+        buf, sem, val = held(row[i])
+        g.tensor.wait_ge(sem, val)
+        mm = g.tensor.matmul(T.acc[:, :], T.ws[:, TILE * i:TILE * (i + 1)], buf[:, :], k == 0, k == len(order) - 1)
+    mm.then_inc(S.mm, 1)
+    g.vector.wait_ge(S.mm, 1)
+    g.vector.tensor_copy(T.ys[:, :], T.acc[:, :]).then_inc(S.cp, 1)
+    g.sync.wait_ge(S.cp, 1)
+    g.sync.dma_start(T.y[:, :], T.ys[:, :]).then_inc(S.st, 16)
+    g.sync.wait_ge(S.st, 16)
+    if sent:
+        g.wait_ge(S.sent, sent)

@@ -30,61 +30,57 @@ def _plan(T, topo):
     cores, need = T.cores, T.tables["MASK"]
     n = len(cores)
     chip = [topo.chip(c) for c in cores]
+    die = [topo.die(c) for c in cores]
     users = {}
     for j in range(n):
         u = [r for r in range(n) if r != j and j in need[r]]
         if u:
             users[j] = u
     far = {j: sorted(set(chip[r] for r in users[j]) - set([chip[j]])) for j in users}
-    gate = {}
-    for ch in sorted(set(chip)):
-        here = [r for r in range(n) if chip[r] == ch]
-        own = [r for r in here if r in users]
-        gate[ch] = min(own, key=lambda r: len(far[r])) if own else here[0]
+    other = {r: [c for c in cores if topo.chip(c) != chip[r]][0] for r in range(n)}
+    away = {r: _bits(topo.mask(cores[r], other[r])) for r in range(n)}
 
-    calls = {r: [] for r in range(n)}
-    count, eta, relay = {}, {}, {r: [] for r in range(n)}
-    turn = 0
+    pend = {r: [] for r in range(n)}
+    count, eta = {}, {}
+
+    def put(f, t, j, ranks, es_all, t_arr):
+        per = len(es_all) // len(ranks)
+        dests = [(r, es_all[q * per:(q + 1) * per]) for q, r in enumerate(ranks)]
+        for r, es in dests:
+            count[(r, j)], eta[(r, j)] = len(es), t_arr
+        pend[f].append((t, j, dests))
+
+    def home(f, r):
+        return [e for e in _bits(topo.mask(cores[f], cores[r])) if e not in away[f]]
+
+    gated = set()
     for j in sorted(users, key=lambda j: -len(far[j])):
-        src = cores[j]
         near = [r for r in users[j] if chip[r] == chip[j]]
-        out = []
-        if far[j]:
-            out = _bits(topo.mask(src, cores[[r for r in users[j] if chip[r] != chip[j]][0]]))
-        cold = [ch for ch in far[j] if gate[ch] not in users]
-        warm = [ch for ch in far[j] if gate[ch] in users]
-        k = (WAVE * turn) % len(cold) if cold else 0
-        order = cold[k:] + cold[:k] + warm
-        turn += 1
-        for w in range(0, len(order), WAVE):
-            wave = order[w:w + WAVE]
-            per = len(out) // len(wave)
-            dests = []
-            for q, ch in enumerate(wave):
-                there = [r for r in users[j] if chip[r] == ch]
-                first = gate[ch] if gate[ch] in there else there[0]
-                es = out[q * per:(q + 1) * per]
-                dests.append((first, es))
-                count[(first, j)], eta[(first, j)] = len(es), 2.0 * (w // WAVE + 1)
-                rest = [r for r in there if r != first]
-                if rest:
-                    relay[first].append((eta[(first, j)], j, rest))
-            calls[j].append((j, dests))
+        at = {ch: sorted((r for r in users[j] if chip[r] == ch), key=lambda r: die[r] != die[j]) for ch in far[j]}
+        helper = near[0] if near and len(far[j]) > WAVE else None
+        fresh = [ch for ch in far[j] if ch not in gated and not any(r in users for r in at[ch])]
+        warm = [ch for ch in far[j] if any(r in users for r in at[ch])]
+        rest = [ch for ch in far[j] if ch not in fresh and ch not in warm]
+        order = fresh + warm + rest
+        first = order[:WAVE] if helper is not None else order
+        second = [ch for ch in far[j] if ch not in first]
+        put(j, 0.0, j, [at[ch][0] for ch in first], away[j], 2.0 if len(first) > 1 else 1.0)
+        for ch in first:
+            gt = at[ch][0]
+            if at[ch][1:]:
+                gated.add(ch)
+                busy = gt in users or any(gt in users[k] and chip[gt] == chip[k] and len(far[k]) > WAVE for k in users)
+                for r in at[ch][1:]:
+                    es = home(gt, r) if busy else _bits(topo.mask(cores[gt], cores[r]))
+                    put(gt, 2.0, j, [r], es, 4.5 if busy else 5.0)
         for r in near:
-            es = [e for e in _bits(topo.mask(src, cores[r])) if e not in out]
-            calls[j].append((j, [(r, es)]))
-            count[(r, j)], eta[(r, j)] = len(es), 3.0
-    for f in range(n):
-        t = 0.0
-        for e0, j, rest in sorted(relay[f]):
-            t = max(t, e0) + 2.0
-            for r in rest:
-                es = _bits(topo.mask(cores[f], cores[r]))
-                if f in far and len(far[f]) > 1:
-                    busy = _bits(topo.mask(cores[f], cores[[u for u in users[f] if chip[u] != chip[f]][0]]))
-                    es = [e for e in es if e not in busy]
-                calls[f].append((j, [(r, es)]))
-                count[(r, j)], eta[(r, j)] = len(es), t
+            put(j, 0.1, j, [r], home(j, r), 1.5)
+        if second:
+            put(j, 0.2, j, [at[ch][0] for ch in second], away[j], 4.0)
+            left = [r for ch in second for r in at[ch][1:]]
+            if left:
+                put(helper, 1.5, j, left, away[helper], 4.5 if helper in users else 5.5)
+    calls = {r: [(j, d) for _, j, d in sorted(pend[r], key=lambda c: c[0])] for r in range(n)}
     return calls, count, eta
 
 

@@ -2,6 +2,7 @@ from concourse.bass import DstId, RemoteDMATransfer
 
 TILE = 128
 WAVE = 2
+NH = 2
 
 SCRATCH = {
     "xs": ("sbuf", [128, 512], "bfloat16"),
@@ -10,9 +11,10 @@ SCRATCH = {
     "l1": ("sbuf", [128, 512], "bfloat16"),
     "l2": ("sbuf", [128, 512], "bfloat16"),
     "ys": ("sbuf", [128, 512], "bfloat16"),
-    "acc": ("psum", [128, 512], "float32"),
+    "acc0": ("psum", [128, 512], "float32"),
+    "acc1": ("psum", [128, 512], "float32"),
 }
-SEMAPHORES = ["ldx", "ldw", "a0", "a1", "a2", "sent", "mm", "cp", "st"]
+SEMAPHORES = ["ldx", "ldw", "a00", "a01", "a10", "a11", "a20", "a21", "sent", "mm0", "mm1", "cp0", "cp1", "st0", "st1"]
 
 
 def _bits(m):
@@ -40,15 +42,16 @@ def _plan(T, topo):
     other = {r: [c for c in cores if topo.chip(c) != chip[r]][0] for r in range(n)}
     away = {r: _bits(topo.mask(cores[r], other[r])) for r in range(n)}
 
-    pend = {r: [] for r in range(n)}
-    count, eta = {}, {}
+    pend = {r: {} for r in range(n)}
+    info = {}
 
-    def put(f, t, j, ranks, es_all, t_arr):
+    def put(f, t, j, p, ranks, es_all, t_arr):
         per = len(es_all) // len(ranks)
-        dests = [(r, es_all[q * per:(q + 1) * per]) for q, r in enumerate(ranks)]
-        for r, es in dests:
-            count[(r, j)], eta[(r, j)] = len(es), t_arr
-        pend[f].append((t, j, dests))
+        for q, r in enumerate(ranks):
+            es = es_all[q * per:(q + 1) * per]
+            for h in (range(NH) if p is None else [p]):
+                info[(r, j, h)] = (0 if p is None else p, len(es), t_arr)
+            pend[f].setdefault(t, []).append((j, p, r, es))
 
     def home(f, r):
         return [e for e in _bits(topo.mask(cores[f], cores[r])) if e not in away[f]]
@@ -57,31 +60,35 @@ def _plan(T, topo):
     for j in sorted(users, key=lambda j: -len(far[j])):
         near = [r for r in users[j] if chip[r] == chip[j]]
         at = {ch: sorted((r for r in users[j] if chip[r] == ch), key=lambda r: die[r] != die[j]) for ch in far[j]}
-        helper = near[0] if near and len(far[j]) > WAVE else None
+        if not (near and len(far[j]) > WAVE):
+            put(j, 0.0, j, None, [r for ch in far[j] for r in at[ch]], away[j], 1.0)
+            for r in near:
+                put(j, 0.1, j, None, [r], home(j, r), 1.0)
+            continue
+        helper = near[0]
         fresh = [ch for ch in far[j] if ch not in gated and not any(r in users for r in at[ch])]
         warm = [ch for ch in far[j] if any(r in users for r in at[ch])]
         rest = [ch for ch in far[j] if ch not in fresh and ch not in warm]
-        order = fresh + warm + rest
-        first = order[:WAVE] if helper is not None else order
+        first = (fresh + rest + warm)[:WAVE]
         second = [ch for ch in far[j] if ch not in first]
-        put(j, 0.0, j, [at[ch][0] for ch in first], away[j], 2.0 if len(first) > 1 else 1.0)
-        for ch in first:
-            gt = at[ch][0]
-            if at[ch][1:]:
+        late = 0.0 if helper in users else 0.3
+        put(j, 0.0, j, None, [at[ch][0] for ch in first], away[j], 2.0)
+        for p in range(NH):
+            for ch in first:
+                gt = at[ch][0]
+                busy = gt in users or any(gt in users[k] and chip[gt] == chip[k] for k in users)
                 gated.add(ch)
-                busy = gt in users or any(gt in users[k] and chip[gt] == chip[k] and len(far[k]) > WAVE for k in users)
                 for r in at[ch][1:]:
                     es = home(gt, r) if busy else _bits(topo.mask(cores[gt], cores[r]))
-                    put(gt, 2.0, j, [r], es, 4.5 if busy else 5.0)
-        for r in near:
-            put(j, 0.1, j, [r], home(j, r), 1.5)
-        if second:
-            put(j, 0.2, j, [at[ch][0] for ch in second], away[j], 4.0)
+                    put(gt, 2.0 + 0.1 * p, j, p, [r], es, 3.6 + 0.35 * p)
+            for r in near:
+                put(j, 0.1 * (p + 1), j, p, [r], home(j, r), 0.6 + 0.5 * p)
+            put(j, 0.1 * (p + 2), j, p, [at[ch][0] for ch in second], away[j], 3.0 + p)
             left = [r for ch in second for r in at[ch][1:]]
             if left:
-                put(helper, 1.5, j, left, away[helper], 4.5 if helper in users else 5.5)
-    calls = {r: [(j, d) for _, j, d in sorted(pend[r], key=lambda c: c[0])] for r in range(n)}
-    return calls, count, eta
+                put(helper, 0.6 + 0.5 * p, j, p, left, away[helper], 2.8 + late + p)
+    calls = {r: [pend[r][t] for t in sorted(pend[r])] for r in range(n)}
+    return calls, info
 
 
 def rank_program(g, core, T, topo):
@@ -91,43 +98,59 @@ def rank_program(g, core, T, topo):
     S = T.sem
     need = T.tables["MASK"]
     row = need[rank]
-    calls, count, eta = _plan(T, topo)
+    calls, info = _plan(T, topo)
+    cw = T.xs.shape[1] // NH
 
-    def held(j):
+    def held(j, h):
         if j == rank:
-            return T.xs, S.ldx, 16
+            return T.xs, "ldx", 16
         i = row.index(j)
-        return T["l%d" % i], S["a%d" % i], count[(rank, j)]
+        return T["l%d" % i], "a%d%d" % (i, info[(rank, j, h)][0]), info[(rank, j, h)][1]
+
+    def wait_once(q, seen, name, val):
+        if name not in seen:
+            seen.add(name)
+            q.wait_ge(S[name], val)
 
     g.sync.dma_start(T.xs[:, :], T.x[:, :]).then_inc(S.ldx, 16)
     g.sync.wait_ge(S.ldx, 16)
     g.sync.dma_start(T.ws[:, :], T.w[:, :]).then_inc(S.ldw, 16)
 
-    sent = 0
-    for j, dests in calls[rank]:
-        buf, sem, val = held(j)
-        g.wait_ge(sem, val)
+    sent, seen = 0, set()
+    for call in calls[rank]:
         trs = []
-        for r, es in dests:
+        for j, p, r, es in call:
+            lo, hi = (0, NH * cw) if p is None else (p * cw, (p + 1) * cw)
+            for h in (range(NH) if p is None else [p]):
+                buf, name, val = held(j, h)
+                wait_once(g, seen, name, val)
             assert topo.may_write(core, T.cores[r])
             rid, pid, _ = topo.addr(T.cores[r])
             i = need[r].index(j)
             trs.append(RemoteDMATransfer(dst_ids=[DstId(rid=rid, pnc=pid)], dma_engine_mask=_mask(es),
-                                         remote_sem=S["a%d" % i], src=buf[:, :], dst=T["l%d" % i][:, :]))
+                                         remote_sem=S["a%d%d" % (i, info[(r, j, 0 if p is None else p)][0])],
+                                         src=buf[:, lo:hi], dst=T["l%d" % i][:, lo:hi]))
             sent += len(es)
         g.remote_dma_fused(trs, local_sem=S.sent)
 
-    order = sorted(range(len(row)), key=lambda i: 0.0 if row[i] == rank else eta[(rank, row[i])])
+    todo = sorted((0.0 if row[i] == rank else info[(rank, row[i], h)][2], h, i)
+                  for i in range(len(row)) for h in range(NH))
+    done, seen = [0] * NH, set()
     g.tensor.wait_ge(S.ldw, 16)
-    for k, i in enumerate(order):
-        buf, sem, val = held(row[i])
-        g.tensor.wait_ge(sem, val)
-        mm = g.tensor.matmul(T.acc[:, :], T.ws[:, TILE * i:TILE * (i + 1)], buf[:, :], k == 0, k == len(order) - 1)
-    mm.then_inc(S.mm, 1)
-    g.vector.wait_ge(S.mm, 1)
-    g.vector.tensor_copy(T.ys[:, :], T.acc[:, :]).then_inc(S.cp, 1)
-    g.sync.wait_ge(S.cp, 1)
-    g.sync.dma_start(T.y[:, :], T.ys[:, :]).then_inc(S.st, 16)
-    g.sync.wait_ge(S.st, 16)
+    for _, h, i in todo:
+        buf, name, val = held(row[i], h)
+        wait_once(g.tensor, seen, name, val)
+        done[h] += 1
+        mm = g.tensor.matmul(T["acc%d" % h][:, 0:cw], T.ws[:, TILE * i:TILE * (i + 1)],
+                             buf[:, h * cw:(h + 1) * cw], done[h] == 1, done[h] == len(row))
+        if done[h] == len(row):
+            mm.then_inc(S["mm%d" % h], 1)
+    for h in range(NH):
+        dq = g.sync if h == 0 else g.scalar
+        g.vector.wait_ge(S["mm%d" % h], 1)
+        g.vector.tensor_copy(T.ys[:, h * cw:(h + 1) * cw], T["acc%d" % h][:, 0:cw]).then_inc(S["cp%d" % h], 1)
+        dq.wait_ge(S["cp%d" % h], 1)
+        dq.dma_start(T.y[:, h * cw:(h + 1) * cw], T.ys[:, h * cw:(h + 1) * cw]).then_inc(S["st%d" % h], 16)
+        dq.wait_ge(S["st%d" % h], 16)
     if sent:
         g.wait_ge(S.sent, sent)

from concourse.bass import DstId, RemoteDMATransfer

TILE = 128
WAVE = 2
NH = 2

SCRATCH = {
    "xs": ("sbuf", [128, 512], "bfloat16"),
    "ws": ("sbuf", [128, 384], "bfloat16"),
    "l0": ("sbuf", [128, 512], "bfloat16"),
    "l1": ("sbuf", [128, 512], "bfloat16"),
    "l2": ("sbuf", [128, 512], "bfloat16"),
    "ys": ("sbuf", [128, 512], "bfloat16"),
    "acc0": ("psum", [128, 512], "float32"),
    "acc1": ("psum", [128, 512], "float32"),
}
SEMAPHORES = ["ldx", "ldw", "a00", "a01", "a10", "a11", "a20", "a21", "sent", "mm0", "mm1", "cp0", "cp1", "st0", "st1"]


def _bits(m):
    return [e for e in range(m.bit_length()) if (m >> e) & 1]


def _mask(es):
    m = 0
    for e in es:
        m |= 1 << e
    return m


def _plan(T, topo):
    cores, need = T.cores, T.tables["MASK"]
    n = len(cores)
    chip = [topo.chip(c) for c in cores]
    die = [topo.die(c) for c in cores]
    users = {}
    for j in range(n):
        u = [r for r in range(n) if r != j and j in need[r]]
        if u:
            users[j] = u
    far = {j: sorted(set(chip[r] for r in users[j]) - set([chip[j]])) for j in users}
    other = {r: [c for c in cores if topo.chip(c) != chip[r]][0] for r in range(n)}
    away = {r: _bits(topo.mask(cores[r], other[r])) for r in range(n)}

    pend = {r: {} for r in range(n)}
    info = {}

    def put(f, t, j, p, ranks, es_all, t_arr):
        per = len(es_all) // len(ranks)
        for q, r in enumerate(ranks):
            es = es_all[q * per:(q + 1) * per]
            for h in (range(NH) if p is None else [p]):
                info[(r, j, h)] = (0 if p is None else p, len(es), t_arr)
            pend[f].setdefault(t, []).append((j, p, r, es))

    def home(f, r):
        return [e for e in _bits(topo.mask(cores[f], cores[r])) if e not in away[f]]

    gated = set()
    for j in sorted(users, key=lambda j: -len(far[j])):
        near = [r for r in users[j] if chip[r] == chip[j]]
        at = {ch: sorted((r for r in users[j] if chip[r] == ch), key=lambda r: die[r] != die[j]) for ch in far[j]}
        if not (near and len(far[j]) > WAVE):
            put(j, 0.0, j, None, [r for ch in far[j] for r in at[ch]], away[j], 1.0)
            for r in near:
                put(j, 0.1, j, None, [r], home(j, r), 1.0)
            continue
        helper = near[0]
        fresh = [ch for ch in far[j] if ch not in gated and not any(r in users for r in at[ch])]
        warm = [ch for ch in far[j] if any(r in users for r in at[ch])]
        rest = [ch for ch in far[j] if ch not in fresh and ch not in warm]
        first = (fresh + rest + warm)[:WAVE]
        second = [ch for ch in far[j] if ch not in first]
        late = 0.0 if helper in users else 0.3
        put(j, 0.0, j, None, [at[ch][0] for ch in first], away[j], 2.0)
        for p in range(NH):
            for ch in first:
                gt = at[ch][0]
                busy = gt in users or any(gt in users[k] and chip[gt] == chip[k] for k in users)
                gated.add(ch)
                for r in at[ch][1:]:
                    es = home(gt, r) if busy else _bits(topo.mask(cores[gt], cores[r]))
                    put(gt, 2.0 + 0.1 * p, j, p, [r], es, 3.6 + 0.35 * p)
            for r in near:
                put(j, 0.1 * (p + 1), j, p, [r], home(j, r), 0.6 + 0.5 * p)
            put(j, 0.1 * (p + 2), j, p, [at[ch][0] for ch in second], away[j], 3.0 + p)
            left = [r for ch in second for r in at[ch][1:]]
            if left:
                put(helper, 0.6 + 0.5 * p, j, p, left, away[helper], 2.8 + late + p)
    calls = {r: [pend[r][t] for t in sorted(pend[r])] for r in range(n)}
    return calls, info


def rank_program(g, core, T, topo):
    rank = T.rank_of(core)
    if rank is None:
        return
    S = T.sem
    need = T.tables["MASK"]
    row = need[rank]
    calls, info = _plan(T, topo)
    cw = T.xs.shape[1] // NH

    def held(j, h):
        if j == rank:
            return T.xs, "ldx", 16
        i = row.index(j)
        return T["l%d" % i], "a%d%d" % (i, info[(rank, j, h)][0]), info[(rank, j, h)][1]

    def wait_once(q, seen, name, val):
        if name not in seen:
            seen.add(name)
            q.wait_ge(S[name], val)

    g.sync.dma_start(T.xs[:, :], T.x[:, :]).then_inc(S.ldx, 16)
    g.sync.wait_ge(S.ldx, 16)
    g.sync.dma_start(T.ws[:, :], T.w[:, :]).then_inc(S.ldw, 16)

    sent, seen = 0, set()
    for call in calls[rank]:
        trs = []
        for j, p, r, es in call:
            lo, hi = (0, NH * cw) if p is None else (p * cw, (p + 1) * cw)
            for h in (range(NH) if p is None else [p]):
                buf, name, val = held(j, h)
                wait_once(g, seen, name, val)
            assert topo.may_write(core, T.cores[r])
            rid, pid, _ = topo.addr(T.cores[r])
            i = need[r].index(j)
            trs.append(RemoteDMATransfer(dst_ids=[DstId(rid=rid, pnc=pid)], dma_engine_mask=_mask(es),
                                         remote_sem=S["a%d%d" % (i, info[(r, j, 0 if p is None else p)][0])],
                                         src=buf[:, lo:hi], dst=T["l%d" % i][:, lo:hi]))
            sent += len(es)
        g.remote_dma_fused(trs, local_sem=S.sent)

    todo = sorted((0.0 if row[i] == rank else info[(rank, row[i], h)][2], h, i)
                  for i in range(len(row)) for h in range(NH))
    done, seen = [0] * NH, set()
    g.tensor.wait_ge(S.ldw, 16)
    for _, h, i in todo:
        buf, name, val = held(row[i], h)
        wait_once(g.tensor, seen, name, val)
        done[h] += 1
        mm = g.tensor.matmul(T["acc%d" % h][:, 0:cw], T.ws[:, TILE * i:TILE * (i + 1)],
                             buf[:, h * cw:(h + 1) * cw], done[h] == 1, done[h] == len(row))
        if done[h] == len(row):
            mm.then_inc(S["mm%d" % h], 1)
    for h in range(NH):
        dq = g.sync if h == 0 else g.scalar
        g.vector.wait_ge(S["mm%d" % h], 1)
        g.vector.tensor_copy(T.ys[:, h * cw:(h + 1) * cw], T["acc%d" % h][:, 0:cw]).then_inc(S["cp%d" % h], 1)
        dq.wait_ge(S["cp%d" % h], 1)
        dq.dma_start(T.y[:, h * cw:(h + 1) * cw], T.ys[:, h * cw:(h + 1) * cw]).then_inc(S["st%d" % h], 16)
        dq.wait_ge(S["st%d" % h], 16)
    if sent:
        g.wait_ge(S.sent, sent)
